import numpy as np
import ml_dtypes


def mxq(x, axis, fmt="e4m3"):
    dtype, down = {"e4m3": (ml_dtypes.float8_e4m3fn, 7), "e5m2": (ml_dtypes.float8_e5m2, 14)}[fmt]
    v = np.moveaxis(np.asarray(x, np.float32).astype(ml_dtypes.bfloat16).astype(np.float64), axis, -1)
    blocks = v.reshape(v.shape[:-1] + (-1, 32))
    amax = np.abs(blocks).max(-1, keepdims=True)
    byte = np.maximum(np.where(amax > 0, np.frexp(amax)[1] - 1 + 127, 0) - down, 1)
    scale = np.exp2(byte - 127.0)
    codes = (blocks / scale).astype(np.float32).astype(dtype).astype(np.float64)
    return np.moveaxis((codes * scale).reshape(v.shape), -1, axis)


WIDE = False


def mx_kscale(k):
    if not WIDE:
        return np.ones(k)
    levels = np.array([10, -10, 5, -5, 0])
    if k % 512:
        return np.exp2(np.random.permutation(np.resize(levels, k // 32))).repeat(32)
    a = np.empty((k // 512, 16))
    for p in range(k // 512):
        a[p, :8] = np.random.permutation(np.resize(levels, 8))
        for g in range(8):
            far = levels[np.abs(levels - a[p, g]) >= 10]
            a[p, g + 8] = far[np.random.randint(len(far))]
    return np.exp2(a.ravel()).repeat(32)


BF16 = ml_dtypes.bfloat16


def bf(x):
    return np.asarray(x, np.float32).astype(BF16)


def f64(x):
    return np.asarray(x).astype(np.float64)


E2M1 = np.array([0.0, 0.5, 1.0, 1.5, 2.0, 3.0, 4.0, 6.0, -0.0, -0.5, -1.0, -1.5, -2.0, -3.0, -4.0, -6.0])


def pack_weight(w, fmt):
    k, n = w.shape
    w = f64(bf(w)).reshape(k // 32, 32, n)
    amax = np.abs(w).max(1)
    if fmt == "e4m3":
        byte = np.frexp(amax)[1] - 1 + 127 - 7
    else:
        mant, ex = np.frexp(amax / 6.0)
        byte = np.where(mant > 0.5, ex, ex - 1) + 127
    byte = np.clip(np.where(amax > 0, byte, 1), 1, 254)
    scaled = (w * np.exp2(127.0 - byte)[:, None, :]).reshape(k, n).astype(np.float32)
    by_word = np.ascontiguousarray(scaled.reshape(k // 512, 128, 4, n).transpose(0, 1, 3, 2))
    if fmt == "e4m3":
        words = by_word.astype(ml_dtypes.float8_e4m3fn).view(np.uint8)
    else:
        c = by_word.astype(ml_dtypes.float4_e2m1fn).view(np.uint8) & 0xF
        words = c[..., 0::2] | (c[..., 1::2] << 4)
    return np.ascontiguousarray(words), np.ascontiguousarray(byte.astype(np.uint8).reshape(k // 512, 16, n))


def unpack_weight(words, scales, fmt):
    g, p, n, _ = words.shape
    if fmt == "e4m3":
        vals = np.ascontiguousarray(words).view(ml_dtypes.float8_e4m3fn).astype(np.float64)
    else:
        nib = np.empty((g, p, n, 4), np.uint8)
        nib[..., 0::2] = words & 0xF
        nib[..., 1::2] = words >> 4
        vals = E2M1[nib]
    vals = vals * np.repeat(np.exp2(scales.astype(np.float64) - 127.0), 8, axis=1)[..., None]
    return vals.transpose(0, 1, 3, 2).reshape(g * 512, n)


N, D, F = 512, 512, 1024


def erf(a):
    c = np.clip(a, -6.0, 6.0)
    term = c
    total = c
    for n in range(1, 150):
        term = term * (2.0 * c * c / (2 * n + 1))
        total = total + term
    r = 2.0 / np.sqrt(np.pi) * np.exp(-c * c) * total
    return np.where(np.abs(a) > 6.0, np.sign(a), r)


def gelu_and_slope(g):
    phi = 0.5 * (1.0 + erf(g / np.sqrt(2.0)))
    act = g * phi
    dact = phi + g * np.exp(-(g * g) / 2.0) / np.sqrt(2.0 * np.pi)
    return act, dact


def draw0():
    s, t = mx_kscale(D), mx_kscale(F)
    cd, cf = 1.0 / np.sqrt(D), 1.0 / np.sqrt(F)
    x = bf(np.random.standard_normal((N, D)) * s)
    wg_words, wg_scales = pack_weight(np.random.standard_normal((D, F)) * cd / s[:, None], "e4m3")
    vg = bf(np.random.standard_normal((D, F)) * cd / s[:, None])
    wu_words, wu_scales = pack_weight(np.random.standard_normal((D, F)) * cd / s[:, None] * t, "e4m3")
    vu = bf(np.random.standard_normal((D, F)) * cd / s[:, None] * t)
    wd_words, wd_scales = pack_weight(np.random.standard_normal((F, D)) * cf / t[:, None], "e4m3")
    vd = bf(np.random.standard_normal((F, D)) * cf / t[:, None])
    return {
        "x": x,
        "wg_words": wg_words,
        "wg_scales": wg_scales,
        "vg": vg,
        "wu_words": wu_words,
        "wu_scales": wu_scales,
        "vu": vu,
        "wd_words": wd_words,
        "wd_scales": wd_scales,
        "vd": vd,
    }


def core(x, wg_words, wg_scales, vg, wu_words, wu_scales, vu, wd_words, wd_scales, vd):
    xq = mxq(f64(x), 1, "e4m3")
    g = xq @ unpack_weight(wg_words, wg_scales, "e4m3")
    dg = xq @ mxq(f64(vg), 0, "e4m3")
    u = xq @ unpack_weight(wu_words, wu_scales, "e4m3")
    du = xq @ mxq(f64(vu), 0, "e4m3")
    act, dact = gelu_and_slope(g)
    h = act * u
    dh = dact * dg * u + act * du
    dy = (mxq(dh, 1, "e4m3") @ unpack_weight(wd_words, wd_scales, "e4m3")) + (mxq(h, 1, "e4m3") @ mxq(f64(vd), 0, "e4m3"))
    return dy


def e4m3fn_bytes(y):
    return np.clip(np.asarray(y, np.float64), -448.0, 448.0).astype(np.float32).astype(ml_dtypes.float8_e4m3fn).view(np.uint8)


def e4m3fn_values(b):
    return np.asarray(b, np.uint8).view(ml_dtypes.float8_e4m3fn).astype(np.float64)


def setup_inputs():
    d = draw0()
    x0 = np.asarray(d['vg']).astype(np.float64)
    s = (np.max(np.abs(x0), axis=(1,), keepdims=True) / 448.0).astype(np.float32)
    out = {}
    for k, v in d.items():
        if k == 'vg':
            out['vg_bytes'] = e4m3fn_bytes(x0 / s.astype(np.float64))
            out['vg_scale'] = s
        else:
            out[k] = v
    return out


def reference(x, wg_words, wg_scales, vg_bytes, vg_scale, wu_words, wu_scales, vu, wd_words, wd_scales, vd):
    return core(x, wg_words, wg_scales, e4m3fn_values(vg_bytes) * vg_scale.astype(np.float64), wu_words, wu_scales, vu, wd_words, wd_scales, vd)

import math
from contextlib import ExitStack

import concourse.mybir as mybir
from concourse.masks import make_identity

N, D, F = 512, 512, 1024
FLOPS = 6 * 2 * N * D * F

F32 = mybir.dt.float32
BF16 = mybir.dt.bfloat16
I32 = mybir.dt.int32
U8 = mybir.dt.uint8
FP8 = mybir.dt.float8_e4m3fn
FP8X4 = mybir.dt.float8_e4m3fn_x4
ACT = mybir.ActivationFunctionType
ALU = mybir.AluOpType

P = 128
PACK = 4
K_PASS = P * PACK
HALVES = F // K_PASS
TILES = N // P
PAIRS = HALVES * TILES // 2
EPS = 2.0**-64
LOG_PDF = -0.5 * math.log(2.0 * math.pi)


def tile_forwardgradientgegluweighttangent_w8_kernel(
    tc, x, wg_words, wg_scales, vg_bytes, vg_scale, wu_words, wu_scales, vu, wd_words, wd_scales, vd, out
):
    nc = tc.nc
    with ExitStack() as ctx:
        keep = ctx.enter_context(tc.tile_pool(name="keep", bufs=1))
        work = ctx.enter_context(tc.tile_pool(name="work", bufs=3))
        banks = ctx.enter_context(tc.psum_pool(name="banks", bufs=4))
        turns = ctx.enter_context(tc.psum_pool(name="turns", bufs=2))
        edge = ctx.enter_context(tc.psum_pool(name="edge", bufs=2))
        ctx.enter_context(tc.manual_schedule())

        def kept(name, count, shape, dtype):
            return [keep.tile(shape, dtype, name="%s%d" % (name, i), align_bytes=64) for i in range(count)]

        x_rows = kept("x_rows", TILES, [P, D], BF16)
        x_grouped = kept("x_grouped", TILES, [P, K_PASS], BF16)
        x_codes = kept("x_codes", TILES, [P, P], I32)
        x_sc = kept("x_sc", TILES, [P, P], U8)
        codes = {w: kept(w + "_codes", HALVES, [P, K_PASS], I32) for w in ("wg", "wu", "vg", "vu", "wd", "vd")}
        made_sc = {w: kept(w + "_sc", HALVES, [P, K_PASS], U8) for w in ("vg", "vu", "vd")}
        given_sc = {w: kept(w + "_sc", 1, [P, F], U8)[0] for w in ("wg", "wu", "wd")}
        vg_fp8 = kept("vg_fp8", HALVES, [P, PACK, K_PASS], U8)
        vg_rowscale = kept("vg_rowscale", 1, [P, PACK], F32)[0]
        rows = {w: kept(w + "_rows", HALVES, [P, PACK, K_PASS], BF16) for w in ("vg", "vu", "vd")}
        grouped = {w: kept(w + "_grouped", HALVES, [P, PACK * K_PASS], BF16) for w in ("vg", "vu", "vd")}
        act = kept("act", PAIRS, [P, 2 * K_PASS], F32)
        sq = kept("sq", PAIRS, [P, 2 * K_PASS], F32)
        inv = kept("inv", PAIRS, [P, 2 * K_PASS], F32)
        even = kept("even", PAIRS, [P, 2 * K_PASS], F32)
        act_du = kept("act_du", PAIRS, [P, 2 * K_PASS], F32)
        slope = kept("slope", PAIRS, [P, 2 * K_PASS], F32)
        h_rows = kept("h_rows", PAIRS, [P, 2 * K_PASS], BF16)
        hid = {w: kept(w, PAIRS, [P, 2 * K_PASS], BF16) for w in ("h", "dh")}
        hid_codes = {w: kept(w + "_codes", PAIRS, [P, 2 * P], I32) for w in ("h", "dh")}
        hid_sc = {w: kept(w + "_sc", PAIRS, [P, 2 * P], U8) for w in ("h", "dh")}
        ident = kept("ident", 1, [P, P], F32)[0]
        warm = kept("warm", 2, [P, 1], F32)

        def cols(i):
            return slice(i * K_PASS, (i + 1) * K_PASS)

        def scale_plane(w, half):
            return made_sc[w][half][:] if w in made_sc else given_sc[w][:, cols(half)]

        def load_x(j):
            nc.sync.dma_start(out=x_rows[j][:], in_=x[j * P : (j + 1) * P, :])

        def load_words(w, half, src):
            nc.sync.dma_start(out=codes[w][half][:], in_=src.rearrange("p n t -> p (n t)").bitcast(I32))

        def load_scales(w, src):
            for q in range(4):
                nc.sync.dma_start(
                    out=given_sc[w][32 * q : 32 * q + 4, :].bitcast(I32), in_=src[0, 4 * q : 4 * q + 4, :].bitcast(I32)
                )

        def load_rows(dst, src):
            nc.sync.dma_start(out=dst[:], in_=src.rearrange("(p j) c -> p j c", j=PACK))

        nc.vector.memset(given_sc["wg"][:].bitcast(I32), 0)
        nc.vector.memset(warm[0][:], 0.0)
        nc.vector.memset(given_sc["wu"][:].bitcast(I32), 0)
        nc.vector.memset(given_sc["wd"][:].bitcast(I32), 0)
        make_identity(nc, ident[:])
        nc.scalar.activation(out=warm[1][:], in_=warm[0][:], func=ACT.Gelu)

        load_x(0)
        load_scales("wg", wg_scales)
        load_words("wg", 0, wg_words[0][:, cols(0), :])
        load_x(1)
        load_words("wg", 1, wg_words[0][:, cols(1), :])
        nc.sync.dma_start(out=vg_rowscale[:], in_=vg_scale.rearrange("(p j) o -> p (j o)", j=PACK))
        load_rows(vg_fp8[0], vg_bytes[:, cols(0)])
        load_x(2)
        load_rows(rows["vu"][0], vu[:, cols(0)])
        load_x(3)
        load_rows(vg_fp8[1], vg_bytes[:, cols(1)])
        load_scales("wu", wu_scales)
        load_words("wu", 0, wu_words[0][:, cols(0), :])
        load_rows(rows["vu"][1], vu[:, cols(1)])
        load_words("wu", 1, wu_words[0][:, cols(1), :])
        for half in range(HALVES):
            load_rows(rows["vd"][half], vd[cols(half), :])
        for half in range(HALVES):
            load_words("wd", half, wd_words[half])
        for q in range(4):
            nc.sync.dma_start(
                out=given_sc["wd"][32 * q : 32 * q + 4, :].bitcast(I32).rearrange("r (g n) -> r g n", g=HALVES),
                in_=wd_scales[:, 4 * q : 4 * q + 4, :].bitcast(I32).rearrange("g r n -> r g n"),
            )

        def turn_x(j):
            bank = turns.tile([P, 2, P], F32, name="x_turned", tag="turn")
            words = x_rows[j][:].bitcast(F32)
            for u in range(2):
                nc.tensor.transpose(bank[:, u, :], words[:, u : 2 * P : 2], ident[:])
            nc.vector.tensor_copy(
                out=x_grouped[j][:].bitcast(F32).rearrange("p (r u) -> p r u", u=2),
                in_=bank[:].rearrange("p u r -> p r u"),
            )

        def quantize(dst_codes, dst_sc, src):
            nc.vector.quantize_mx(out=dst_codes.bitcast(FP8X4), scales=dst_sc, in_=src)

        def quantize_x(j):
            quantize(x_codes[j][:], x_sc[j][:], x_grouped[j][:])

        def quantize_dir(w, half):
            quantize(codes[w][half][:], made_sc[w][half][:], grouped[w][half][:])

        def group(eng, w, half, part_no=0, parts=1):
            cs = slice(part_no * K_PASS // parts, (part_no + 1) * K_PASS // parts)
            dst = grouped[w][half][:].rearrange("p (c j) -> p c j", j=PACK)[:, cs]
            src = rows[w][half][:].rearrange("p j c -> p c j")[:, cs]
            if eng is nc.gpsimd:
                eng.tensor_scalar(out=dst, in0=src, scalar1=1.0, scalar2=0.0, op0=ALU.mult, op1=ALU.add)
            elif eng is nc.scalar:
                eng.copy(out=dst, in_=src)
            else:
                eng.tensor_copy(out=dst, in_=src)

        def widen_vg(eng, half):
            for j in range(PACK):
                dst, src, factor = rows["vg"][half][:, j, :], vg_fp8[half][:, j, :].bitcast(FP8), vg_rowscale[:, j : j + 1]
                if eng is nc.scalar:
                    eng.activation(out=dst, in_=src, func=ACT.Copy, scale=factor)
                else:
                    eng.tensor_scalar(out=dst, in0=src, scalar1=factor, scalar2=None, op0=ALU.mult)

        ready = {}

        def project_raw(w, j, half):
            return ready.pop((w, j, half)) if (w, j, half) in ready else issue(w, j, half)

        def ahead(w, j, half):
            ready[(w, j, half)] = issue(w, j, half)

        def issue(w, j, half):
            bank = banks.tile([P, K_PASS], F32, name="proj", tag="proj")
            nc.tensor.matmul_mx(
                out=bank[:],
                lhsT=x_codes[j][:].bitcast(FP8X4), lhsT_scale=x_sc[j][:],
                rhs=codes[w][half][:].bitcast(FP8X4), rhs_scale=scale_plane(w, half),
                start=True, stop=True,
            )
            return bank[:]

        def project(w, j, half):
            return project_raw(w, j, half).rearrange("p (m t) -> p t m", t=PACK)

        def flat(tiles, j, half):
            return tiles[j][:, cols(half)]

        def part(tiles, j, half):
            return flat(tiles, j, half).rearrange("p (t m) -> p t m", t=PACK)

        def gate(j, half):
            g = project("wg", j, half)
            nc.scalar.activation(out=part(sq, j, half), in_=g, func=ACT.Square)
            nc.scalar.activation(out=part(act, j, half), in_=g, func=ACT.Gelu)

        def even_part(j, half):
            g = project("wg", j, half)
            nc.vector.scalar_tensor_tensor(
                out=part(even, j, half), in0=g, scalar=-0.5, in1=part(act, j, half), op0=ALU.mult, op1=ALU.add
            )

        def log_sq(k):
            nc.scalar.activation(out=inv[k][:], in_=sq[k][:], func=ACT.Ln, bias=EPS)

        def exp_inv(k):
            nc.scalar.activation(out=inv[k][:], in_=inv[k][:], func=ACT.Exp, scale=-1.0)

        def exp_pdf(k):
            nc.scalar.activation(out=sq[k][:], in_=sq[k][:], func=ACT.Exp, scale=-0.5, bias=LOG_PDF)

        def make_h(j, half):
            u = project_raw("wu", j, half)
            nc.vector.tensor_tensor(
                out=flat(h_rows, j, half).rearrange("p (u m e) -> p u m e", u=2, e=2),
                in0=u.rearrange("p (m u e) -> p u m e", u=2, e=2),
                in1=flat(act, j, half).rearrange("p (u e m) -> p u m e", u=2, e=2),
                op=ALU.mult,
            )

        def make_q(j, half):
            du = project("vu", j, half)
            nc.vector.tensor_tensor(out=part(act_du, j, half), in0=du, in1=part(act, j, half), op=ALU.mult)

        def turn_h(k):
            bank = turns.tile([P, 2, 2, P], F32, name="h_turned", tag="turn")
            words = h_rows[k][:].bitcast(F32).rearrange("p (j u m) -> p j u m", j=2, u=2)
            for jj in range(2):
                for u in range(2):
                    nc.tensor.transpose(bank[:, jj, u, :], words[:, jj, u, :], ident[:])
            nc.scalar.copy(
                out=hid["h"][k][:].bitcast(F32).rearrange("p (j r u) -> p j r u", j=2, u=2),
                in_=bank[:].rearrange("p j u r -> p j r u"),
            )

        def turn_dh(j, half):
            bank = turns.tile([P, PACK, P], F32, name="dh_turned", tag="turn")
            for t in range(PACK):
                for i, term in enumerate((act_du, slope)):
                    nc.tensor.matmul(
                        out=bank[:, t, :], lhsT=part(term, j, half)[:, t, :], rhs=ident[:],
                        is_transpose=True, start=(i == 0), stop=(i == 1),
                    )
            nc.scalar.copy(
                out=flat(hid["dh"], j, half).rearrange("p (r t) -> p r t", t=PACK),
                in_=bank[:].rearrange("p t r -> p r t"),
            )

        def quantize_hid(w, k):
            quantize(hid_codes[w][k][:], hid_sc[w][k][:], hid[w][k][:])

        def quantize_dh_step(k, jj):
            m = slice(jj * P, (jj + 1) * P)
            quantize(hid_codes["dh"][k][:, m], hid_sc["dh"][k][:, m], hid["dh"][k][:, cols(jj)])

        def odd_scale(eng, k):
            eng.tensor_tensor(out=even[k][:], in0=even[k][:], in1=inv[k][:], op=ALU.mult)

        def odd_add(eng, k, lo=0, hi=2):
            cs = slice(lo * K_PASS, hi * K_PASS)
            eng.tensor_tensor(out=even[k][:, cs], in0=even[k][:, cs], in1=sq[k][:, cs], op=ALU.add)

        def times_g(j, half):
            g = project("wg", j, half)
            nc.vector.tensor_tensor(out=part(slope, j, half), in0=g, in1=part(even, j, half), op=ALU.mult)

        def times_dg(j, half):
            dg = project("vg", j, half)
            nc.vector.scalar_tensor_tensor(
                out=part(slope, j, half), in0=part(slope, j, half), scalar=0.5, in1=dg, op0=ALU.add, op1=ALU.mult
            )

        def times_u(j, half):
            u = project("wu", j, half)
            nc.vector.tensor_tensor(out=part(slope, j, half), in0=u, in1=part(slope, j, half), op=ALU.mult)

        acc = {}

        def down_pass(j, w, half, first=False, last=False):
            if first:
                acc[j] = edge.tile([P, D], F32, name="down", tag="edge")
            k, m = j, slice(half * P, (half + 1) * P)
            weight = "vd" if w == "h" else "wd"
            nc.tensor.matmul_mx(
                out=acc[j][:],
                lhsT=hid_codes[w][k][:, m].bitcast(FP8X4), lhsT_scale=hid_sc[w][k][:, m],
                rhs=codes[weight][half][:].bitcast(FP8X4), rhs_scale=scale_plane(weight, half),
                start=first, stop=last,
            )

        def down_open(j):
            down_pass(j, "h", 0, first=True)
            down_pass(j, "h", 1)

        def down_close(j):
            down_pass(j, "dh", 0)
            down_pass(j, "dh", 1, last=True)

        def store(eng, j):
            result = work.tile([P, D], F32, name="result")
            if eng is nc.scalar:
                eng.copy(out=result[:], in_=acc[j][:])
            else:
                eng.tensor_copy(out=result[:], in_=acc[j][:])
            nc.sync.dma_start(out=out[j * P : (j + 1) * P, :], in_=result[:])

        V, A, G = nc.vector, nc.scalar, nc.gpsimd
        turn_x(0)
        quantize_x(0)
        gate(0, 0)
        turn_x(1)
        gate(0, 1)
        quantize_x(1)
        gate(1, 0)
        gate(1, 1)
        widen_vg(V, 0)
        turn_x(2)
        quantize_x(2)
        gate(2, 0)
        gate(2, 1)
        group(V, "vu", 0, 0, 1)
        turn_x(3)
        quantize_x(3)
        quantize_dir("vu", 0)
        gate(3, 0)
        gate(3, 1)
        log_sq(0)
        log_sq(1)
        log_sq(2)
        log_sq(3)
        exp_inv(0)
        exp_pdf(0)
        exp_inv(1)
        exp_pdf(1)
        exp_inv(2)
        exp_pdf(2)
        exp_inv(3)
        exp_pdf(3)
        group(V, "vg", 0, 0, 1)
        widen_vg(V, 1)
        quantize_dir("vg", 0)
        group(G, "vg", 1, 0, 1)
        group(G, "vu", 1, 0, 1)
        even_part(0, 0)
        even_part(0, 1)
        make_h(0, 0)
        make_q(0, 0)
        make_h(1, 0)
        make_q(1, 0)
        even_part(1, 0)
        make_h(2, 0)
        make_q(2, 0)
        make_h(3, 0)
        make_q(3, 0)
        quantize_dir("vg", 1)
        quantize_dir("vu", 1)
        group(V, "vd", 0, 0, 1)
        make_h(0, 1)
        quantize_dir("vd", 0)
        odd_scale(V, 0)
        make_q(0, 1)
        odd_add(V, 0)
        group(A, "vd", 1, 0, 1)
        even_part(1, 1)
        odd_scale(G, 1)
        odd_add(G, 1)
        times_g(0, 0)
        times_g(0, 1)
        even_part(2, 0)
        times_dg(0, 0)
        times_dg(0, 1)
        make_h(1, 1)
        times_u(0, 0)
        times_u(0, 1)
        make_q(1, 1)
        make_h(2, 1)
        quantize_dir("vd", 1)
        even_part(2, 1)
        odd_scale(G, 2)
        odd_add(G, 2)
        times_g(1, 0)
        times_g(1, 1)
        turn_dh(0, 0)
        turn_dh(0, 1)
        make_h(3, 1)
        times_dg(1, 0)
        times_dg(1, 1)
        turn_h(0)
        turn_h(1)
        even_part(3, 0)
        times_u(1, 0)
        times_u(1, 1)
        make_q(2, 1)
        quantize_hid("dh", 0)
        quantize_hid("h", 0)
        quantize_hid("h", 1)
        even_part(3, 1)
        odd_scale(G, 3)
        odd_add(G, 3)
        times_g(2, 0)
        times_g(2, 1)
        turn_dh(1, 0)
        turn_dh(1, 1)
        times_dg(2, 0)
        times_dg(2, 1)
        turn_h(2)
        turn_h(3)
        times_u(2, 0)
        times_u(2, 1)
        make_q(3, 1)
        down_open(0)
        down_close(0)
        store(A, 0)
        quantize_hid("dh", 1)
        quantize_hid("h", 2)
        quantize_hid("h", 3)
        times_g(3, 0)
        times_g(3, 1)
        turn_dh(2, 0)
        turn_dh(2, 1)
        times_dg(3, 0)
        ahead("vg", 3, 1)
        down_open(1)
        down_close(1)
        store(A, 1)
        quantize_hid("dh", 2)
        times_dg(3, 1)
        ahead("wu", 3, 0)
        ahead("wu", 3, 1)
        down_open(2)
        down_close(2)
        store(A, 2)
        times_u(3, 0)
        down_open(3)
        turn_dh(3, 0)
        times_u(3, 1)
        turn_dh(3, 1)
        quantize_dh_step(3, 0)
        quantize_dh_step(3, 1)
        down_close(3)
        store(V, 3)
